import numpy as np
import ml_dtypes


def mxq(x, axis, fmt="e4m3"):
    dtype, down = {"e4m3": (ml_dtypes.float8_e4m3fn, 7), "e5m2": (ml_dtypes.float8_e5m2, 14)}[fmt]
    v = np.moveaxis(np.asarray(x, np.float32).astype(ml_dtypes.bfloat16).astype(np.float64), axis, -1)
    blocks = v.reshape(v.shape[:-1] + (-1, 32))
    amax = np.abs(blocks).max(-1, keepdims=True)
    byte = np.maximum(np.where(amax > 0, np.frexp(amax)[1] - 1 + 127, 0) - down, 1)
    scale = np.exp2(byte - 127.0)
    codes = (blocks / scale).astype(np.float32).astype(dtype).astype(np.float64)
    return np.moveaxis((codes * scale).reshape(v.shape), -1, axis)


WIDE = False


def mx_kscale(k):
    if not WIDE:
        return np.ones(k)
    levels = np.array([10, -10, 5, -5, 0])
    if k % 512:
        return np.exp2(np.random.permutation(np.resize(levels, k // 32))).repeat(32)
    a = np.empty((k // 512, 16))
    for p in range(k // 512):
        a[p, :8] = np.random.permutation(np.resize(levels, 8))
        for g in range(8):
            far = levels[np.abs(levels - a[p, g]) >= 10]
            a[p, g + 8] = far[np.random.randint(len(far))]
    return np.exp2(a.ravel()).repeat(32)


def f64(x):
    return np.asarray(x).astype(np.float64)


def striped(idx):
    return np.tile(idx.reshape(-1, 16).T, (8, 1)).astype(np.uint16)


def unstriped(offs):
    return offs[:16].T.reshape(-1).astype(np.int64)


def striped8(idx):
    return np.concatenate([x.reshape(-1, 16).T for x in idx]).astype(np.uint16)


def runs(offs, k):
    lists = np.stack([offs[16 * r : 16 * r + 16].T.reshape(-1) for r in range(8)]).astype(np.int64)
    return lists[np.arange(k) % 512 // 64]


def pack_weight(w):
    k, n = w.shape
    w = f64(np.asarray(w, np.float32).astype(ml_dtypes.bfloat16)).reshape(k // 32, 32, n)
    amax = np.abs(w).max(1)
    byte = np.clip(np.where(amax > 0, np.frexp(amax)[1] - 1 + 127 - 7, 1), 1, 254)
    scaled = (w * np.exp2(127.0 - byte)[:, None, :]).reshape(k, n).astype(np.float32)
    words = np.ascontiguousarray(scaled.reshape(k // 512, 128, 4, n).transpose(0, 1, 3, 2)).astype(ml_dtypes.float8_e4m3fn).view(np.uint8)
    return words, np.ascontiguousarray(byte.astype(np.uint8).reshape(k // 512, 16, n))


def unpack_weight(words, scales):
    g, p, n, _ = words.shape
    vals = np.ascontiguousarray(words).view(ml_dtypes.float8_e4m3fn).astype(np.float64) * np.repeat(np.exp2(scales.astype(np.float64) - 127.0), 8, axis=1)[..., None]
    return vals.transpose(0, 1, 3, 2).reshape(g * 512, n)


def sigmoid(v):
    return 1.0 / (1.0 + np.exp(-np.maximum(v, -700.0)))

def planes(y):
    n, m = y.shape
    v = y.astype(np.float32).astype(ml_dtypes.bfloat16).astype(np.float64).reshape(n // 32, 32, m)
    top = np.abs(v).max(1)
    byte = np.clip(np.where(top > 0, np.frexp(top)[1] - 1 + 127 - 7, 1), 1, 254)
    codes = (v * np.exp2(127.0 - byte)[:, None, :]).reshape(n, m).astype(np.float32).astype(ml_dtypes.float8_e4m3fn).view(np.uint8)
    words = codes.reshape(n // 512, 128, 4, m).transpose(0, 1, 3, 2)
    return np.ascontiguousarray(words), np.ascontiguousarray(byte.astype(np.uint8).reshape(n // 512, 16, m))


K, T, S, G, H, U = 512, 2048, 512, 2048, 512, 1024


def setup_inputs():
    n = np.random.standard_normal
    s = mx_kscale(K)[:, None]
    packed_xT = pack_weight(n((K, T)) * s)
    packed_dT = pack_weight(n((K, G)) / s)
    return {
        "x_words": packed_xT[0],
        "x_scales": packed_xT[1],
        "d_words": packed_dT[0],
        "d_scales": packed_dT[1],
        "gs": (np.random.uniform(0.5, 1.5, (K, 1)) * s).astype(np.float32),
        "mem": n((H, U)).astype(np.float32),
        "offs": striped(np.random.permutation(T)[:S]),
        "k1": striped8(np.random.randint(0, G, (8, H))),
        "n1": striped8(np.stack([np.random.permutation(S) for _ in range(8)])),
        "n2": striped8(np.stack([np.random.permutation(S) for _ in range(8)])),
        "n3": striped8(np.stack([np.random.permutation(U)[:S] for _ in range(8)])),
    }


def reference(x_words, x_scales, d_words, d_scales, gs, mem, offs, k1, n1, n2, n3):
    old = f64(mem)[np.arange(H)[:, None], runs(n3, H)]
    d_k1 = unpack_weight(d_words, d_scales)[np.arange(K)[:, None], runs(k1, K)]
    xq = unpack_weight(x_words, x_scales)[:, unstriped(offs)]
    h = 0.0625 * (d_k1.T @ xq)
    z = f64(gs) * (h - (np.minimum(h[np.arange(H)[:, None], runs(n1, H)], h[np.arange(H)[:, None], runs(n2, H)])))
    h2 = 0.0625 * ((d_k1.T @ mxq(z, 0, "e4m3")))
    nw = old + sigmoid(h2) * (h2 - old)
    out = f64(mem).copy()
    out[np.arange(H)[:, None], runs(n3, H)] = nw
    return (out,) + planes(out)

from contextlib import ExitStack

import concourse.mybir as mybir

K, T, S, G, H, U = 512, 2048, 512, 2048, 512, 1024
FLOPS = 2 * 2 * K * H * S

F32 = mybir.dt.float32
BF16 = mybir.dt.bfloat16
I32 = mybir.dt.int32
U32 = mybir.dt.uint32
U16 = mybir.dt.uint16
U8 = mybir.dt.uint8
FP8X4 = mybir.dt.float8_e4m3fn_x4
ACT = mybir.ActivationFunctionType
ALU = mybir.AluOpType

P = 128
PACK = 4
HALF = S // 2
LIST_COLS = S // 16
SIXTEENTH = 0.0625
ORDER = (0, 2, 3, 1)


def tile_picked_ringunderpaget_none_po_kernel(
    tc, x_words, x_scales, d_words, d_scales, gs, mem, offs, k1, n1, n2, n3, out_0, out_1, out_2
):
    nc = tc.nc
    with ExitStack() as ctx:
        lists = ctx.enter_context(tc.tile_pool(name="lists", bufs=1))
        keep = ctx.enter_context(tc.tile_pool(name="keep", bufs=1))
        psum = ctx.enter_context(tc.psum_pool(name="psum", bufs=1))

        def load_list(dram, name):
            tile = lists.tile([P, LIST_COLS], U16, name=name)
            nc.sync.dma_start(tile[:], dram)
            return tile

        def list_half(tile, half):
            return tile[:, half * LIST_COLS // 2 : (half + 1) * LIST_COLS // 2]

        def cols(half):
            return slice(half * HALF, (half + 1) * HALF)

        k1_sb = load_list(k1, "k1_sb")
        d_scale_table = keep.tile([P, G], U8, name="d_scale_table")
        nc.sync.dma_start(
            d_scale_table[:].bitcast(I32),
            d_scales[0].bitcast(I32).unsqueeze(1).to_broadcast([16, 8, G // 4]),
        )
        offs_sb = load_list(offs, "offs_sb")
        n3_sb = load_list(n3, "n3_sb")
        gs_sb = keep.tile([P, PACK], F32, name="gs_sb")
        nc.gpsimd.dma_start(gs_sb[:], gs.rearrange("(p t) o -> p (t o)", t=PACK))
        d_word_table = keep.tile([P, G], I32, name="d_word_table", tag="slot1")
        nc.sync.dma_start(d_word_table[:], d_words[0].rearrange("p c r -> p (c r)").bitcast(I32))
        x_word_table = keep.tile([P, T], I32, name="x_word_table", tag="slot3")
        nc.sync.dma_start(x_word_table[:], x_words[0].rearrange("p c r -> p (c r)").bitcast(I32))
        n1_sb = load_list(n1, "n1_sb")
        n2_sb = load_list(n2, "n2_sb")

        x_scale_table = keep.tile([P, T], U8, name="x_scale_table", tag="slot0")
        nc.vector.memset(x_scale_table[:].bitcast(I32), 0)
        for q in range(4):
            nc.scalar.dma_start(
                x_scale_table[32 * q : 32 * q + 4, :].bitcast(I32), x_scales[0, 4 * q : 4 * q + 4, :].bitcast(I32)
            )

        mem_rows = mem.rearrange("(p t) c -> p t c", t=PACK)
        out_rows = out_0.rearrange("(p t) c -> p t c", t=PACK)

        gs16 = keep.tile([P, PACK], F32, name="gs16")
        nc.scalar.activation(gs16[:], gs_sb[:], ACT.Copy, scale=SIXTEENTH)

        d_scale_picked = keep.tile([P, H], U8, name="d_scale_picked")
        nc.vector.tensor_copy(d_scale_picked[:], d_scale_table[:].indirect(k1_sb[:]))
        d_scale_dealt = keep.tile([P, H], U8, name="d_scale_dealt", tag="slot2")
        nc.vector.tensor_copy(
            d_scale_dealt[:].rearrange("p (t m) -> p m t", t=PACK),
            d_scale_picked[:].rearrange("p (m t) -> p m t", t=PACK),
        )
        d_scale = keep.tile([P, H], U8, name="d_scale", align_bytes=64)
        nc.vector.memset(d_scale[:].bitcast(I32), 0)
        for r in range(4):
            nc.scalar.dma_start(d_scale[r:P:32, :].bitcast(I32), d_scale_dealt[8 * r : P : 32, :].bitcast(I32))

        x_scale = keep.tile([P, S], U8, name="x_scale", align_bytes=64)
        nc.vector.tensor_copy(x_scale[:], x_scale_table[:].indirect(offs_sb[:]))

        d_picked = keep.tile([P, H], U32, name="d_picked")
        nc.vector.tensor_copy(d_picked[:], d_word_table[:].bitcast(U32).indirect(k1_sb[:]))
        d_codes = keep.tile([P, H], U32, name="d_codes", align_bytes=64)
        nc.vector.tensor_copy(
            d_codes[:].rearrange("p (t m) -> p m t", t=PACK),
            d_picked[:].rearrange("p (m t) -> p m t", t=PACK),
        )
        x_codes = [keep.tile([P, HALF], U32, name=f"x_codes{half}", align_bytes=64) for half in range(2)]
        for half in range(2):
            nc.vector.tensor_copy(x_codes[half][:], x_word_table[:].bitcast(U32).indirect(list_half(offs_sb, half)))

        page = [keep.tile([P, U], F32, name=f"page{t}", tag=f"slot{ORDER.index(t)}") for t in range(PACK)]
        for t in ORDER:
            nc.sync.dma_start(page[t][:], mem_rows[:, t, :])

        def product(out, t, codes, scale):
            rows = slice(t * P, (t + 1) * P)
            nc.tensor.matmul_mx(
                out=out,
                lhsT=d_codes[:, rows].bitcast(FP8X4),
                lhsT_scale=d_scale[:, rows],
                rhs=codes.bitcast(FP8X4),
                rhs_scale=scale,
                start=True,
                stop=True,
            )

        h_bank = [[psum.tile([P, 2, HALF], F32, name=f"h_bank{half}{pair}") for pair in range(2)] for half in range(2)]
        neg_h = [keep.tile([P, S], F32, name=f"neg_h{t}") for t in range(PACK)]
        gs_h = keep.tile([P, PACK, S], F32, name="gs_h")
        for half in range(2):
            for t in range(PACK):
                product(h_bank[half][t // 2][:, t % 2, :], t, x_codes[half][:], x_scale[:, cols(half)])
        for t in range(PACK):
            for half in range(2):
                nc.scalar.activation(neg_h[t][:, cols(half)], h_bank[half][t // 2][:, t % 2, :], ACT.Copy, scale=-1.0)
        for half in range(2):
            for t in range(PACK):
                nc.scalar.activation(
                    gs_h[:, t, cols(half)], h_bank[half][t // 2][:, t % 2, :], ACT.Copy, scale=gs16[:, t : t + 1]
                )

        keep_old = keep.tile([P, PACK, S], F32, name="keep_old")
        fresh = keep.tile([P, PACK, S], F32, name="fresh")
        z_grouped = [None, None]

        def make_z(half):
            neg_min = keep.tile([P, PACK, HALF], F32, name=f"neg_min{half}")
            for pair in range(2):
                tag = "grouped0" if (half, pair) == (1, 1) else f"looked{half}{pair}"
                looked = keep.tile([P, 2, 2, HALF], F32, name=f"looked{half}{pair}", tag=tag, align_bytes=64)
                for i in range(2):
                    window = neg_h[2 * pair + i]
                    nc.vector.tensor_copy(looked[:, 0, i, :], window[:].indirect(list_half(n1_sb, half)))
                    nc.vector.tensor_copy(looked[:, 1, i, :], window[:].indirect(list_half(n2_sb, half)))
                nc.vector.tensor_tensor(neg_min[:, 2 * pair : 2 * pair + 2, :], looked[:, 0], looked[:, 1], ALU.max)
            z_planes = keep.tile([P, PACK, HALF], BF16, name=f"z_planes{half}")
            for t in range(PACK):
                nc.vector.scalar_tensor_tensor(
                    z_planes[:, t, :], neg_min[:, t, :], gs16[:, t : t + 1], gs_h[:, t, cols(half)], ALU.mult, ALU.add
                )
            z_grouped[half] = keep.tile([P, HALF, PACK], BF16, name=f"z_grouped{half}", tag=f"grouped{half}", align_bytes=64)
            nc.scalar.copy(z_grouped[half][:], z_planes[:].rearrange("p t c -> p c t"))

        def second_product(half):
            z_codes = keep.tile([P, HALF], U32, name=f"z_codes{half}", align_bytes=64)
            z_scale = keep.tile([P, HALF], U8, name=f"z_scale{half}", align_bytes=64)
            nc.vector.quantize_mx(
                out=z_codes[:].bitcast(FP8X4), scales=z_scale[:], in_=z_grouped[half][:].rearrange("p c t -> p (c t)")
            )
            for pair in range(2):
                bank = psum.tile([P, 2, HALF], F32, name=f"h2_bank{half}{pair}")
                for i in range(2):
                    product(bank[:, i, :], ORDER[2 * pair + i], z_codes[:], z_scale[:])
                tanh = keep.tile([P, 2, HALF], F32, name=f"tanh{half}{pair}")
                ts = slice(2 * pair, 2 * pair + 2)
                nc.scalar.activation(tanh[:], bank[:], ACT.Tanh, scale=-SIXTEENTH / 2)
                nc.scalar.activation(keep_old[:, ts, cols(half)], tanh[:], ACT.Copy, scale=0.5, bias=0.5)
                nc.scalar.activation(fresh[:, ts, cols(half)], bank[:], ACT.Silu, scale=SIXTEENTH)

        def write_slots(turn, offsets, columns, kept):
            window = page[ORDER[turn]]
            nc.vector.tensor_tensor(kept[:], window[:].indirect(offsets), keep_old[:, turn, columns], ALU.mult)
            nc.vector.tensor_tensor(window[:].indirect(offsets), kept[:], fresh[:, turn, columns], ALU.add)

        out_grouped = [keep.tile([P, U // 2, PACK], BF16, name=f"out_grouped{side}", align_bytes=64) for side in range(2)]

        def hand_out(t):
            nc.sync.dma_start(out_rows[:, t, :], page[t][:])
            for side in range(2):
                source = page[t][:, side * U // 2 : (side + 1) * U // 2]
                if t == ORDER[-1] and side == 0:
                    nc.vector.tensor_copy(out_grouped[side][:, :, t], source)
                else:
                    nc.scalar.copy(out_grouped[side][:, :, t], source)

        make_z(0)
        second_product(0)
        make_z(1)
        write_slots(0, list_half(n3_sb, 0), cols(0), keep.tile([P, HALF], F32, name="kept00"))
        second_product(1)
        write_slots(1, list_half(n3_sb, 0), cols(0), keep.tile([P, HALF], F32, name="kept10", tag="grouped1", align_bytes=64))
        for turn in range(2):
            write_slots(turn, list_half(n3_sb, 1), cols(1), keep.tile([P, HALF], F32, name=f"kept{turn}1"))
            hand_out(ORDER[turn])
        write_slots(2, n3_sb[:], slice(0, S), keep.tile([P, S], F32, name="kept2"))
        hand_out(ORDER[2])
        write_slots(3, n3_sb[:], slice(0, S), keep.tile([P, S], F32, name="kept3", tag="slot0"))
        hand_out(ORDER[3])

        out_codes = [keep.tile([P, U // 2], I32, name=f"out_codes{side}", align_bytes=64) for side in range(2)]
        out_scale = keep.tile([P, U], U8, name="out_scale", align_bytes=64)
        words_out = out_1[0].rearrange("p c r -> p (c r)").bitcast(I32)
        for side in range(2):
            side_cols = slice(side * U // 2, (side + 1) * U // 2)
            nc.vector.quantize_mx(
                out=out_codes[side][:].bitcast(FP8X4),
                scales=out_scale[:, side_cols],
                in_=out_grouped[side][:].rearrange("p c t -> p (c t)"),
            )
            nc.sync.dma_start(words_out[:, side_cols], out_codes[side][:])
        for q in range(4):
            queue = nc.scalar if q % 2 else nc.sync
            queue.dma_start(
                out_2[0, 4 * q : 4 * q + 4, :].bitcast(I32), out_scale[32 * q : 32 * q + 4, :].bitcast(I32)
            )
